import numpy as np
CORES = [2,10,130,138,258,266,386,394]
N = 8
def setup_inputs(rng):
    return {"x": rng.standard_normal((N, 128, 512), dtype=np.float32)}
def reference(x):
    s = x.sum(axis=0, dtype=np.float64).astype(x.dtype)
    s = np.maximum(s, 0)
    return {"y": np.broadcast_to(s, (N,) + s.shape)}

@@ -1,0 +1,91 @@
+from concourse.bass import DstId, RemoteDMATransfer
+from concourse.mybir import AluOpType
+
+W = 128
+
+SCRATCH = {
+    "xs": ("sbuf", [128, 512], "float32"),
+    "l1": ("sbuf", [128, 384], "float32"),
+    "l2": ("sbuf", [128, 128], "float32"),
+    "pa": ("sbuf", [128, 128], "float32"),
+    "pb": ("sbuf", [128, 128], "float32"),
+    "p": ("sbuf", [128, 128], "float32"),
+    "res": ("sbuf", [128, 512], "float32"),
+    "zero": ("psum", [128, 128], "float32"),
+}
+SEMAPHORES = ["ld", "s1", "s2", "s3_0", "s3_1", "s3_2", "s3_3", "sent",
+              "vz", "v1", "v2", "v3", "r0", "r1", "r2", "r3", "stored"]
+
+
+def rank_program(g, core, T, topo):
+    if T.rank_of(core) is None:
+        return
+    h, c = topo.host(core), topo.chip(core)
+
+    def core_of(hh, cc):
+        return hh * 128 + cc * 8 + 2
+
+    q = 2 * (0 if h in (0, 3) else 1) + c
+    mate, swp, dia, cab = core_of(h, c ^ 1), core_of(h ^ 1, c), core_of(h ^ 1, c ^ 1), core_of(3 - h, c)
+
+    def cols(t, k):
+        return t[:, k * W:(k + 1) * W]
+
+    def dst(d):
+        rid, pid = topo.addr(d, core)
+        return DstId(rid=rid, pnc=pid)
+
+    s3 = [T.sem.s3_0, T.sem.s3_1, T.sem.s3_2, T.sem.s3_3]
+    rl = [T.sem.r0, T.sem.r1, T.sem.r2, T.sem.r3]
+    v, sy = g.vector, g.sync
+
+    sy.dma_start(T.xs[:], T.x[:]).then_inc(T.sem.ld, 16)
+    v.memset(T.zero[:], 0.0).then_inc(T.sem.vz, 1)
+
+    g.wait_ge(T.sem.ld, 16)
+    g.remote_dma_fused([
+        RemoteDMATransfer(dst_ids=[dst(dia)], dma_engine_mask=0x0F, remote_sem=T.sem.s1,
+                          src=cols(T.xs, q ^ 3), dst=cols(T.l1, 2)),
+        RemoteDMATransfer(dst_ids=[dst(swp)], dma_engine_mask=0x30, remote_sem=T.sem.s1,
+                          src=cols(T.xs, q ^ 2), dst=cols(T.l1, 1)),
+        RemoteDMATransfer(dst_ids=[dst(mate)], dma_engine_mask=0xC0, remote_sem=T.sem.s1,
+                          src=cols(T.xs, q ^ 1), dst=cols(T.l1, 0)),
+    ], local_sem=T.sem.sent)
+
+    g.wait_ge(T.sem.s1, 8)
+    g.remote_dma_fused([
+        RemoteDMATransfer(dst_ids=[dst(cab)], dma_engine_mask=0xFF, remote_sem=T.sem.s2,
+                          srcs=[cols(T.xs, q), cols(T.l1, 0), cols(T.l1, 1), cols(T.l1, 2)],
+                          dsts=[T.l2[:]], alu_op=1),
+    ], local_sem=T.sem.sent)
+
+    v.wait_ge(T.sem.ld, 16)
+    v.wait_ge(T.sem.s1, 8)
+    v.tensor_tensor(T.pa[:], cols(T.xs, q), cols(T.l1, 0), AluOpType.add).then_inc(T.sem.v1, 1)
+    v.tensor_tensor(T.pb[:], cols(T.l1, 1), cols(T.l1, 2), AluOpType.add).then_inc(T.sem.v1, 1)
+    v.wait_ge(T.sem.v1, 2)
+    v.tensor_tensor(T.p[:], T.pa[:], T.pb[:], AluOpType.add).then_inc(T.sem.v2, 1)
+
+    g.wait_ge(T.sem.s2, 8)
+    g.wait_ge(T.sem.v2, 1)
+    g.remote_dma_fused([
+        RemoteDMATransfer(dst_ids=[dst(mate), dst(swp), dst(dia)], dma_engine_mask=0xFF, remote_sem=s3[q],
+                          srcs=[T.p[:], T.l2[:]],
+                          dsts=[cols(T.res, q), cols(T.res, q), cols(T.res, q)], alu_op=1),
+    ], local_sem=T.sem.sent)
+
+    v.wait_ge(T.sem.v2, 1)
+    v.wait_ge(T.sem.s2, 8)
+    v.tensor_tensor(cols(T.res, q), T.p[:], T.l2[:], AluOpType.add).then_inc(T.sem.v3, 1)
+    v.wait_ge(T.sem.v3, 1)
+    v.wait_ge(T.sem.vz, 1)
+    v.tensor_tensor(cols(T.res, q), cols(T.res, q), T.zero[:], AluOpType.max).then_inc(rl[q], 1)
+    sy.wait_ge(rl[q], 1)
+    sy.dma_start(cols(T.y, q), cols(T.res, q)).then_inc(T.sem.stored, 16)
+    for k in (q ^ 1, q ^ 2, q ^ 3):
+        v.wait_ge(s3[k], 8)
+        v.tensor_tensor(cols(T.res, k), cols(T.res, k), T.zero[:], AluOpType.max).then_inc(rl[k], 1)
+        sy.wait_ge(rl[k], 1)
+        sy.dma_start(cols(T.y, k), cols(T.res, k)).then_inc(T.sem.stored, 16)
+    sy.wait_ge(T.sem.stored, 64)
+    g.wait_ge(T.sem.sent, 24)

@@ -1,32 +1,33 @@
 from concourse.bass import DstId, RemoteDMATransfer
 from concourse.mybir import AluOpType
 
-W = 128
+W = 64
+HELP = 6
+SPLIT = True
 
 SCRATCH = {
     "xs": ("sbuf", [128, 512], "float32"),
-    "l1": ("sbuf", [128, 384], "float32"),
-    "l2": ("sbuf", [128, 128], "float32"),
-    "pa": ("sbuf", [128, 128], "float32"),
-    "pb": ("sbuf", [128, 128], "float32"),
-    "p": ("sbuf", [128, 128], "float32"),
+    "l1": ("sbuf", [128, 256], "float32"),
+    "l2": ("sbuf", [128, 64], "float32"),
+    "pa": ("sbuf", [128, 64], "float32"),
+    "pb": ("sbuf", [128, 64], "float32"),
+    "p": ("sbuf", [128, 64], "float32"),
     "res": ("sbuf", [128, 512], "float32"),
-    "zero": ("psum", [128, 128], "float32"),
+    "zero": ("psum", [128, 256], "float32"),
 }
-SEMAPHORES = ["ld", "s1", "s2", "s3_0", "s3_1", "s3_2", "s3_3", "sent",
-              "vz", "v1", "v2", "v3", "r0", "r1", "r2", "r3", "stored"]
+SEMAPHORES = ["ld0", "ld1", "s1", "s2", "s3a", "s3b", "sent", "vz", "v1", "v2", "v3", "ra", "rb", "stored"]
 
 
 def rank_program(g, core, T, topo):
-    if T.rank_of(core) is None:
+    h, c, n = topo.host(core), topo.chip(core), core % 8
+    if c > 1 or n not in (2, HELP):
         return
-    h, c = topo.host(core), topo.chip(core)
-
-    def core_of(hh, cc):
-        return hh * 128 + cc * 8 + 2
-
+    j = 0 if n == 2 else 1
     q = 2 * (0 if h in (0, 3) else 1) + c
-    mate, swp, dia, cab = core_of(h, c ^ 1), core_of(h ^ 1, c), core_of(h ^ 1, c ^ 1), core_of(3 - h, c)
+    e = 4 * j + q
+
+    def at(hh, cc, nn):
+        return hh * 128 + cc * 8 + nn
 
     def cols(t, k):
         return t[:, k * W:(k + 1) * W]
@@ -35,57 +36,87 @@ def rank_program(g, core, T, topo):
         rid, pid = topo.addr(d, core)
         return DstId(rid=rid, pnc=pid)
 
-    s3 = [T.sem.s3_0, T.sem.s3_1, T.sem.s3_2, T.sem.s3_3]
-    rl = [T.sem.r0, T.sem.r1, T.sem.r2, T.sem.r3]
     v, sy = g.vector, g.sync
+    sent = 0
 
-    sy.dma_start(T.xs[:], T.x[:]).then_inc(T.sem.ld, 16)
-    v.memset(T.zero[:], 0.0).then_inc(T.sem.vz, 1)
+    if j == 0:
+        sy.dma_start(T.xs[:, 256:512], T.x[:, 256:512]).then_inc(T.sem.ld1, 16)
+        sy.dma_start(T.xs[:, 0:256], T.x[:, 0:256]).then_inc(T.sem.ld0, 16)
+        v.memset(T.zero[:], 0.0).then_inc(T.sem.vz, 1)
 
-    g.wait_ge(T.sem.ld, 16)
+        def s1(jj, md, ms, mm):
+            nn = (2, HELP)[jj]
+            tr = [
+                RemoteDMATransfer(dst_ids=[dst(at(h ^ 1, c ^ 1, nn))], dma_engine_mask=md, remote_sem=T.sem.s1,
+                                  src=cols(T.xs, 4 * jj + (q ^ 3)), dst=cols(T.l1, 2)),
+                RemoteDMATransfer(dst_ids=[dst(at(h ^ 1, c, nn))], dma_engine_mask=ms, remote_sem=T.sem.s1,
+                                  src=cols(T.xs, 4 * jj + (q ^ 2)), dst=cols(T.l1, 1)),
+                RemoteDMATransfer(dst_ids=[dst(at(h, c ^ 1, nn))], dma_engine_mask=mm, remote_sem=T.sem.s1,
+                                  src=cols(T.xs, 4 * jj + (q ^ 1)), dst=cols(T.l1, 0)),
+            ]
+            if jj == 1:
+                tr.append(RemoteDMATransfer(dst_ids=[dst(at(h, c, nn))], dma_engine_mask=0xFF00, remote_sem=T.sem.s1,
+                                            src=cols(T.xs, 4 + q), dst=cols(T.l1, 3)))
+            return tr
+
+        if SPLIT:
+            g.wait_ge(T.sem.ld1, 16)
+            g.remote_dma_fused(s1(1, 0x0F, 0x30, 0xC0), local_sem=T.sem.sent)
+            g.wait_ge(T.sem.ld0, 16)
+            g.remote_dma_fused(s1(0, 0xF0, 0x03, 0x0C), local_sem=T.sem.sent)
+            sent += 24
+        else:
+            g.wait_ge(T.sem.ld1, 16)
+            g.wait_ge(T.sem.ld0, 16)
+            g.remote_dma_fused(s1(1, 0x03, 0x04, 0x08) + s1(0, 0x30, 0x40, 0x80), local_sem=T.sem.sent)
+            sent += 16
+    if SPLIT:
+        n1 = 8 if j == 0 else 16
+    else:
+        n1 = 4 if j == 0 else 12
+    mine = cols(T.xs, e) if j == 0 else cols(T.l1, 3)
+
+    g.wait_ge(T.sem.s1, n1)
     g.remote_dma_fused([
-        RemoteDMATransfer(dst_ids=[dst(dia)], dma_engine_mask=0x0F, remote_sem=T.sem.s1,
-                          src=cols(T.xs, q ^ 3), dst=cols(T.l1, 2)),
-        RemoteDMATransfer(dst_ids=[dst(swp)], dma_engine_mask=0x30, remote_sem=T.sem.s1,
-                          src=cols(T.xs, q ^ 2), dst=cols(T.l1, 1)),
-        RemoteDMATransfer(dst_ids=[dst(mate)], dma_engine_mask=0xC0, remote_sem=T.sem.s1,
-                          src=cols(T.xs, q ^ 1), dst=cols(T.l1, 0)),
-    ], local_sem=T.sem.sent)
-
-    g.wait_ge(T.sem.s1, 8)
-    g.remote_dma_fused([
-        RemoteDMATransfer(dst_ids=[dst(cab)], dma_engine_mask=0xFF, remote_sem=T.sem.s2,
-                          srcs=[cols(T.xs, q), cols(T.l1, 0), cols(T.l1, 1), cols(T.l1, 2)],
+        RemoteDMATransfer(dst_ids=[dst(at(3 - h, c, n))], dma_engine_mask=0xFF, remote_sem=T.sem.s2,
+                          srcs=[mine, cols(T.l1, 0), cols(T.l1, 1), cols(T.l1, 2)],
                           dsts=[T.l2[:]], alu_op=1),
     ], local_sem=T.sem.sent)
+    sent += 8
 
-    v.wait_ge(T.sem.ld, 16)
-    v.wait_ge(T.sem.s1, 8)
-    v.tensor_tensor(T.pa[:], cols(T.xs, q), cols(T.l1, 0), AluOpType.add).then_inc(T.sem.v1, 1)
+    if j == 0:
+        v.wait_ge(T.sem.ld0, 16)
+    v.wait_ge(T.sem.s1, n1)
+    v.tensor_tensor(T.pa[:], mine, cols(T.l1, 0), AluOpType.add).then_inc(T.sem.v1, 1)
     v.tensor_tensor(T.pb[:], cols(T.l1, 1), cols(T.l1, 2), AluOpType.add).then_inc(T.sem.v1, 1)
     v.wait_ge(T.sem.v1, 2)
     v.tensor_tensor(T.p[:], T.pa[:], T.pb[:], AluOpType.add).then_inc(T.sem.v2, 1)
 
+    to = [at(h, c ^ 1, 2), at(h ^ 1, c, 2), at(h ^ 1, c ^ 1, 2)]
+    if j == 1:
+        to = [at(h, c, 2)] + to
     g.wait_ge(T.sem.s2, 8)
     g.wait_ge(T.sem.v2, 1)
     g.remote_dma_fused([
-        RemoteDMATransfer(dst_ids=[dst(mate), dst(swp), dst(dia)], dma_engine_mask=0xFF, remote_sem=s3[q],
-                          srcs=[T.p[:], T.l2[:]],
-                          dsts=[cols(T.res, q), cols(T.res, q), cols(T.res, q)], alu_op=1),
+        RemoteDMATransfer(dst_ids=[dst(d) for d in to], dma_engine_mask=0xFF,
+                          remote_sem=(T.sem.s3a, T.sem.s3b)[j],
+                          srcs=[T.p[:], T.l2[:]], dsts=[cols(T.res, e) for d in to], alu_op=1),
     ], local_sem=T.sem.sent)
+    sent += 8
 
-    v.wait_ge(T.sem.v2, 1)
-    v.wait_ge(T.sem.s2, 8)
-    v.tensor_tensor(cols(T.res, q), T.p[:], T.l2[:], AluOpType.add).then_inc(T.sem.v3, 1)
-    v.wait_ge(T.sem.v3, 1)
-    v.wait_ge(T.sem.vz, 1)
-    v.tensor_tensor(cols(T.res, q), cols(T.res, q), T.zero[:], AluOpType.max).then_inc(rl[q], 1)
-    sy.wait_ge(rl[q], 1)
-    sy.dma_start(cols(T.y, q), cols(T.res, q)).then_inc(T.sem.stored, 16)
-    for k in (q ^ 1, q ^ 2, q ^ 3):
-        v.wait_ge(s3[k], 8)
-        v.tensor_tensor(cols(T.res, k), cols(T.res, k), T.zero[:], AluOpType.max).then_inc(rl[k], 1)
-        sy.wait_ge(rl[k], 1)
-        sy.dma_start(cols(T.y, k), cols(T.res, k)).then_inc(T.sem.stored, 16)
-    sy.wait_ge(T.sem.stored, 64)
-    g.wait_ge(T.sem.sent, 24)
+    if j == 0:
+        v.wait_ge(T.sem.v2, 1)
+        v.wait_ge(T.sem.s2, 8)
+        v.tensor_tensor(cols(T.res, e), T.p[:], T.l2[:], AluOpType.add).then_inc(T.sem.v3, 1)
+        v.wait_ge(T.sem.vz, 1)
+        v.wait_ge(T.sem.s3b, 32)
+        v.tensor_tensor(T.res[:, 256:512], T.res[:, 256:512], T.zero[:], AluOpType.max).then_inc(T.sem.rb, 1)
+        sy.wait_ge(T.sem.rb, 1)
+        sy.dma_start(T.y[:, 256:512], T.res[:, 256:512]).then_inc(T.sem.stored, 16)
+        v.wait_ge(T.sem.v3, 1)
+        v.wait_ge(T.sem.s3a, 24)
+        v.tensor_tensor(T.res[:, 0:256], T.res[:, 0:256], T.zero[:], AluOpType.max).then_inc(T.sem.ra, 1)
+        sy.wait_ge(T.sem.ra, 1)
+        sy.dma_start(T.y[:, 0:256], T.res[:, 0:256]).then_inc(T.sem.stored, 16)
+        sy.wait_ge(T.sem.stored, 32)
+    g.wait_ge(T.sem.sent, sent)

@@ -3,7 +3,6 @@ from concourse.mybir import AluOpType
 
 W = 64
 HELP = 6
-SPLIT = True
 
 SCRATCH = {
     "xs": ("sbuf", [128, 512], "float32"),
@@ -59,21 +58,12 @@ def rank_program(g, core, T, topo):
                                             src=cols(T.xs, 4 + q), dst=cols(T.l1, 3)))
             return tr
 
-        if SPLIT:
-            g.wait_ge(T.sem.ld1, 16)
-            g.remote_dma_fused(s1(1, 0x0F, 0x30, 0xC0), local_sem=T.sem.sent)
-            g.wait_ge(T.sem.ld0, 16)
-            g.remote_dma_fused(s1(0, 0xF0, 0x03, 0x0C), local_sem=T.sem.sent)
-            sent += 24
-        else:
-            g.wait_ge(T.sem.ld1, 16)
-            g.wait_ge(T.sem.ld0, 16)
-            g.remote_dma_fused(s1(1, 0x03, 0x04, 0x08) + s1(0, 0x30, 0x40, 0x80), local_sem=T.sem.sent)
-            sent += 16
-    if SPLIT:
-        n1 = 8 if j == 0 else 16
-    else:
-        n1 = 4 if j == 0 else 12
+        g.wait_ge(T.sem.ld1, 16)
+        g.remote_dma_fused(s1(1, 0x0F, 0x30, 0xC0), local_sem=T.sem.sent)
+        g.wait_ge(T.sem.ld0, 16)
+        g.remote_dma_fused(s1(0, 0xF0, 0x03, 0x0C), local_sem=T.sem.sent)
+        sent += 24
+    n1 = 8 if j == 0 else 16
     mine = cols(T.xs, e) if j == 0 else cols(T.l1, 3)
 
     g.wait_ge(T.sem.s1, n1)
@@ -92,22 +82,24 @@ def rank_program(g, core, T, topo):
     v.wait_ge(T.sem.v1, 2)
     v.tensor_tensor(T.p[:], T.pa[:], T.pb[:], AluOpType.add).then_inc(T.sem.v2, 1)
 
-    to = [at(h, c ^ 1, 2), at(h ^ 1, c, 2), at(h ^ 1, c ^ 1, 2)]
+    away = [at(h, c ^ 1, 2), at(h ^ 1, c, 2), at(h ^ 1, c ^ 1, 2)]
+    arrived = (T.sem.s3a, T.sem.s3b)[j]
+    out = cols(T.res, e)
+    tr = [RemoteDMATransfer(dst_ids=[dst(d) for d in away], dma_engine_mask=0x00FF, remote_sem=arrived,
+                            srcs=[T.p[:], T.l2[:]], dsts=[out for d in away], alu_op=1)]
+    sent += 8
     if j == 1:
-        to = [at(h, c, 2)] + to
+        tr.append(RemoteDMATransfer(dst_ids=[dst(at(h, c, 2))], dma_engine_mask=0xFF00, remote_sem=arrived,
+                                    srcs=[T.p[:], T.l2[:]], dsts=[out], alu_op=1))
+        sent += 8
     g.wait_ge(T.sem.s2, 8)
     g.wait_ge(T.sem.v2, 1)
-    g.remote_dma_fused([
-        RemoteDMATransfer(dst_ids=[dst(d) for d in to], dma_engine_mask=0xFF,
-                          remote_sem=(T.sem.s3a, T.sem.s3b)[j],
-                          srcs=[T.p[:], T.l2[:]], dsts=[cols(T.res, e) for d in to], alu_op=1),
-    ], local_sem=T.sem.sent)
-    sent += 8
+    g.remote_dma_fused(tr, local_sem=T.sem.sent)
 
     if j == 0:
         v.wait_ge(T.sem.v2, 1)
         v.wait_ge(T.sem.s2, 8)
-        v.tensor_tensor(cols(T.res, e), T.p[:], T.l2[:], AluOpType.add).then_inc(T.sem.v3, 1)
+        v.tensor_tensor(out, T.p[:], T.l2[:], AluOpType.add).then_inc(T.sem.v3, 1)
         v.wait_ge(T.sem.vz, 1)
         v.wait_ge(T.sem.s3b, 32)
         v.tensor_tensor(T.res[:, 256:512], T.res[:, 256:512], T.zero[:], AluOpType.max).then_inc(T.sem.rb, 1)

from concourse.bass import DstId, RemoteDMATransfer
from concourse.mybir import AluOpType

W = 64
HELP = 6

SCRATCH = {
    "xs": ("sbuf", [128, 512], "float32"),
    "l1": ("sbuf", [128, 256], "float32"),
    "l2": ("sbuf", [128, 64], "float32"),
    "pa": ("sbuf", [128, 64], "float32"),
    "pb": ("sbuf", [128, 64], "float32"),
    "p": ("sbuf", [128, 64], "float32"),
    "res": ("sbuf", [128, 512], "float32"),
    "zero": ("psum", [128, 256], "float32"),
}
SEMAPHORES = ["ld0", "ld1", "s1", "s2", "s3a", "s3b", "sent", "vz", "v1", "v2", "v3", "ra", "rb", "stored"]


def rank_program(g, core, T, topo):
    h, c, n = topo.host(core), topo.chip(core), core % 8
    if c > 1 or n not in (2, HELP):
        return
    j = 0 if n == 2 else 1
    q = 2 * (0 if h in (0, 3) else 1) + c
    e = 4 * j + q

    def at(hh, cc, nn):
        return hh * 128 + cc * 8 + nn

    def cols(t, k):
        return t[:, k * W:(k + 1) * W]

    def dst(d):
        rid, pid = topo.addr(d, core)
        return DstId(rid=rid, pnc=pid)

    v, sy = g.vector, g.sync
    sent = 0

    if j == 0:
        sy.dma_start(T.xs[:, 256:512], T.x[:, 256:512]).then_inc(T.sem.ld1, 16)
        sy.dma_start(T.xs[:, 0:256], T.x[:, 0:256]).then_inc(T.sem.ld0, 16)
        v.memset(T.zero[:], 0.0).then_inc(T.sem.vz, 1)

        def s1(jj, md, ms, mm):
            nn = (2, HELP)[jj]
            tr = [
                RemoteDMATransfer(dst_ids=[dst(at(h ^ 1, c ^ 1, nn))], dma_engine_mask=md, remote_sem=T.sem.s1,
                                  src=cols(T.xs, 4 * jj + (q ^ 3)), dst=cols(T.l1, 2)),
                RemoteDMATransfer(dst_ids=[dst(at(h ^ 1, c, nn))], dma_engine_mask=ms, remote_sem=T.sem.s1,
                                  src=cols(T.xs, 4 * jj + (q ^ 2)), dst=cols(T.l1, 1)),
                RemoteDMATransfer(dst_ids=[dst(at(h, c ^ 1, nn))], dma_engine_mask=mm, remote_sem=T.sem.s1,
                                  src=cols(T.xs, 4 * jj + (q ^ 1)), dst=cols(T.l1, 0)),
            ]
            if jj == 1:
                tr.append(RemoteDMATransfer(dst_ids=[dst(at(h, c, nn))], dma_engine_mask=0xFF00, remote_sem=T.sem.s1,
                                            src=cols(T.xs, 4 + q), dst=cols(T.l1, 3)))
            return tr

        g.wait_ge(T.sem.ld1, 16)
        g.remote_dma_fused(s1(1, 0x0F, 0x30, 0xC0), local_sem=T.sem.sent)
        g.wait_ge(T.sem.ld0, 16)
        g.remote_dma_fused(s1(0, 0xF0, 0x03, 0x0C), local_sem=T.sem.sent)
        sent += 24
    n1 = 8 if j == 0 else 16
    mine = cols(T.xs, e) if j == 0 else cols(T.l1, 3)

    g.wait_ge(T.sem.s1, n1)
    g.remote_dma_fused([
        RemoteDMATransfer(dst_ids=[dst(at(3 - h, c, n))], dma_engine_mask=0xFF, remote_sem=T.sem.s2,
                          srcs=[mine, cols(T.l1, 0), cols(T.l1, 1), cols(T.l1, 2)],
                          dsts=[T.l2[:]], alu_op=1),
    ], local_sem=T.sem.sent)
    sent += 8

    if j == 0:
        v.wait_ge(T.sem.ld0, 16)
    v.wait_ge(T.sem.s1, n1)
    v.tensor_tensor(T.pa[:], mine, cols(T.l1, 0), AluOpType.add).then_inc(T.sem.v1, 1)
    v.tensor_tensor(T.pb[:], cols(T.l1, 1), cols(T.l1, 2), AluOpType.add).then_inc(T.sem.v1, 1)
    v.wait_ge(T.sem.v1, 2)
    v.tensor_tensor(T.p[:], T.pa[:], T.pb[:], AluOpType.add).then_inc(T.sem.v2, 1)

    away = [at(h, c ^ 1, 2), at(h ^ 1, c, 2), at(h ^ 1, c ^ 1, 2)]
    arrived = (T.sem.s3a, T.sem.s3b)[j]
    out = cols(T.res, e)
    tr = [RemoteDMATransfer(dst_ids=[dst(d) for d in away], dma_engine_mask=0x00FF, remote_sem=arrived,
                            srcs=[T.p[:], T.l2[:]], dsts=[out for d in away], alu_op=1)]
    sent += 8
    if j == 1:
        tr.append(RemoteDMATransfer(dst_ids=[dst(at(h, c, 2))], dma_engine_mask=0xFF00, remote_sem=arrived,
                                    srcs=[T.p[:], T.l2[:]], dsts=[out], alu_op=1))
        sent += 8
    g.wait_ge(T.sem.s2, 8)
    g.wait_ge(T.sem.v2, 1)
    g.remote_dma_fused(tr, local_sem=T.sem.sent)

    if j == 0:
        v.wait_ge(T.sem.v2, 1)
        v.wait_ge(T.sem.s2, 8)
        v.tensor_tensor(out, T.p[:], T.l2[:], AluOpType.add).then_inc(T.sem.v3, 1)
        v.wait_ge(T.sem.vz, 1)
        v.wait_ge(T.sem.s3b, 32)
        v.tensor_tensor(T.res[:, 256:512], T.res[:, 256:512], T.zero[:], AluOpType.max).then_inc(T.sem.rb, 1)
        sy.wait_ge(T.sem.rb, 1)
        sy.dma_start(T.y[:, 256:512], T.res[:, 256:512]).then_inc(T.sem.stored, 16)
        v.wait_ge(T.sem.v3, 1)
        v.wait_ge(T.sem.s3a, 24)
        v.tensor_tensor(T.res[:, 0:256], T.res[:, 0:256], T.zero[:], AluOpType.max).then_inc(T.sem.ra, 1)
        sy.wait_ge(T.sem.ra, 1)
        sy.dma_start(T.y[:, 0:256], T.res[:, 0:256]).then_inc(T.sem.stored, 16)
        sy.wait_ge(T.sem.stored, 32)
    g.wait_ge(T.sem.sent, sent)
